import numpy as np
import ml_dtypes


def mxq(x, axis, fmt="e4m3"):
    dtype, down = {"e4m3": (ml_dtypes.float8_e4m3fn, 7), "e5m2": (ml_dtypes.float8_e5m2, 14)}[fmt]
    v = np.moveaxis(np.asarray(x, np.float32).astype(ml_dtypes.bfloat16).astype(np.float64), axis, -1)
    blocks = v.reshape(v.shape[:-1] + (-1, 32))
    amax = np.abs(blocks).max(-1, keepdims=True)
    byte = np.maximum(np.where(amax > 0, np.frexp(amax)[1] - 1 + 127, 0) - down, 1)
    scale = np.exp2(byte - 127.0)
    codes = (blocks / scale).astype(np.float32).astype(dtype).astype(np.float64)
    return np.moveaxis((codes * scale).reshape(v.shape), -1, axis)


WIDE = False


def mx_kscale(k):
    if not WIDE:
        return np.ones(k)
    levels = np.array([10, -10, 5, -5, 0])
    if k % 512:
        return np.exp2(np.random.permutation(np.resize(levels, k // 32))).repeat(32)
    a = np.empty((k // 512, 16))
    for p in range(k // 512):
        a[p, :8] = np.random.permutation(np.resize(levels, 8))
        for g in range(8):
            far = levels[np.abs(levels - a[p, g]) >= 10]
            a[p, g + 8] = far[np.random.randint(len(far))]
    return np.exp2(a.ravel()).repeat(32)


def f64(x):
    return np.asarray(x).astype(np.float64)


def striped(idx):
    return np.tile(idx.reshape(-1, 16).T, (8, 1)).astype(np.uint16)


def unstriped(offs):
    return offs[:16].T.reshape(-1).astype(np.int64)


E2M1 = np.array([0.0, 0.5, 1.0, 1.5, 2.0, 3.0, 4.0, 6.0, -0.0, -0.5, -1.0, -1.5, -2.0, -3.0, -4.0, -6.0])


def pack_weight(w, fmt):
    k, n = w.shape
    w = f64(np.asarray(w, np.float32).astype(ml_dtypes.bfloat16)).reshape(k // 32, 32, n)
    amax = np.abs(w).max(1)
    if fmt == "e4m3":
        byte = np.frexp(amax)[1] - 1 + 127 - 7
    else:
        mant, ex = np.frexp(amax / 6.0)
        byte = np.where(mant > 0.5, ex, ex - 1) + 127
    byte = np.clip(np.where(amax > 0, byte, 1), 1, 254)
    scaled = (w * np.exp2(127.0 - byte)[:, None, :]).reshape(k, n).astype(np.float32)
    by_word = np.ascontiguousarray(scaled.reshape(k // 512, 128, 4, n).transpose(0, 1, 3, 2))
    if fmt == "e4m3":
        words = by_word.astype(ml_dtypes.float8_e4m3fn).view(np.uint8)
    else:
        c = by_word.astype(ml_dtypes.float4_e2m1fn).view(np.uint8) & 0xF
        words = (c[..., 0::2] | (c[..., 1::2] << 4)).reshape(k // 512, 128, 2 * n)
    return np.ascontiguousarray(words), np.ascontiguousarray(byte.astype(np.uint8).reshape(k // 512, 16, n))


def unpack_weight(words, scales, fmt):
    g, _, n = scales.shape
    words = np.ascontiguousarray(words).reshape(g, 128, n, -1)
    if fmt == "e4m3":
        vals = words.view(ml_dtypes.float8_e4m3fn).astype(np.float64)
    else:
        nib = np.empty((g, 128, n, 4), np.uint8)
        nib[..., 0::2] = words & 0xF
        nib[..., 1::2] = words >> 4
        vals = E2M1[nib]
    vals = vals * np.repeat(np.exp2(scales.astype(np.float64) - 127.0), 8, axis=1)[..., None]
    return vals.transpose(0, 1, 3, 2).reshape(g * 512, n)


def gelu(v):
    return 0.5 * v * (1.0 + np.tanh(np.sqrt(2.0 / np.pi) * (v + 0.044715 * v**3)))


K, H, T, S, P = 1024, 512, 4096, 1024, 512


def setup_inputs():
    n = np.random.standard_normal
    s = mx_kscale(K)[:, None]
    u = mx_kscale(H)[:, None]
    tab_words, tab_scales = pack_weight(n((K, T)) * s, "e4m3")
    w2_words, w2_scales = pack_weight(0.8 * n((K, H)) / np.sqrt(K) / s, "e2m1")
    w4_words, w4_scales = pack_weight(0.8 * n((H, H)) / np.sqrt(H) / u, "e2m1")
    return {
        "tab_words": tab_words, "tab_scales": tab_scales,
        "offs": striped(np.random.permutation(T)[:S]),
        "pos1": striped(np.random.permutation(S)[:P]),
        "w1": (1.3 * n((K, H)) / np.sqrt(K) / s).astype(np.float32),
        "w2_words": w2_words, "w2_scales": w2_scales,
        "gain": (np.exp(0.3 * n(H)) * u[:, 0]).astype(np.float32),
        "timebase": n((H, P)).astype(np.float32),
        "w3": (0.8 * n((H, H)) / np.sqrt(H) / u).astype(np.float32),
        "w4_words": w4_words, "w4_scales": w4_scales,
        "w5": (0.8 * n((K, H)) / np.sqrt(K) / s).astype(np.float32),
        "skip": (np.exp(0.3 * n(H)) / u[:, 0]).astype(np.float32),
        "wgo": np.exp(0.3 * n((128, P))).astype(np.float32),
    }


def reference(tab_words, tab_scales, offs, pos1, w1, w2_words, w2_scales, gain, timebase,
              w3, w4_words, w4_scales, w5, skip, wgo):
    v = unpack_weight(tab_words, tab_scales, "e4m3")[:, unstriped(offs)]
    w2 = unpack_weight(w2_words, w2_scales, "e2m1")
    w4 = unpack_weight(w4_words, w4_scales, "e2m1")
    bent = np.tanh(mxq(f64(w1), 0, "e4m3").T @ v)
    h = (bent + (w2.T @ v)) * f64(gain)[:, None]
    d = mxq(f64(w5), 0, "e4m3").T @ v
    x = h[:, unstriped(pos1)]
    xt = x * f64(timebase)
    y = mxq(f64(w3), 0, "e4m3").T @ mxq(x, 0, "e4m3") + w4.T @ mxq(xt, 0, "e4m3")
    y = np.tanh(y) + d[:, unstriped(pos1)]
    out = f64(skip)[:, None] * h
    out[:, unstriped(pos1)] = np.tile(f64(wgo), (H // 128, 1)) * y
    return out

@@ -1,0 +1,257 @@
+from contextlib import ExitStack
+
+import concourse.mybir as mybir
+
+K, H, T, S, M = 1024, 512, 4096, 1024, 512
+FLOPS = 2 * (3 * K * H * S + 2 * H * H * M)
+
+F32 = mybir.dt.float32
+BF16 = mybir.dt.bfloat16
+I32 = mybir.dt.int32
+U32 = mybir.dt.uint32
+U16 = mybir.dt.uint16
+U8 = mybir.dt.uint8
+FP8X4 = mybir.dt.float8_e4m3fn_x4
+FP4X4 = mybir.dt.float4_e2m1fn_x4
+ADD = mybir.AluOpType.add
+MULT = mybir.AluOpType.mult
+TANH = mybir.ActivationFunctionType.Tanh
+COPY = mybir.ActivationFunctionType.Copy
+
+P = 128
+PACK = 4
+PASSES = K // (P * PACK)
+QUADS = 4
+BANK = 512
+HALVES = S // BANK
+
+
+def tile_list_chroma_line_restorer_kernel(
+    tc, tab_words, tab_scales, offs, pos1, w1, w2_words, w2_scales, gain, timebase,
+    w3, w4_words, w4_scales, w5, skip, wgo, out,
+):
+    nc = tc.nc
+    with ExitStack() as ctx:
+        keep = ctx.enter_context(tc.tile_pool(name="keep", bufs=1))
+        ring = ctx.enter_context(tc.tile_pool(name="ring", bufs=3))
+        psum = ctx.enter_context(tc.psum_pool(name="psum", bufs=4))
+
+        def held(shape, dtype, name):
+            return keep.tile(shape, dtype, name=name, align_bytes=64)
+
+        def load_rows(rows, name):
+            raw = held([P, PACK, H], F32, name)
+            nc.sync.dma_start(out=raw[:], in_=rows.rearrange("(p j) c -> p j c", j=PACK))
+            return raw
+
+        def weave_weight(raw):
+            woven = ring.tile([P, PACK * H], BF16, name="weight_woven", align_bytes=64)
+            nc.scalar.copy(
+                out=woven[:].rearrange("p (t m j) -> p m j t", t=PACK, j=PACK),
+                in_=raw[:].rearrange("p j (m t) -> p m j t", t=PACK),
+            )
+            return woven
+
+        def quantize(woven, name):
+            codes = held([P, BANK], U32, name + "_codes")
+            scales = held([P, BANK], U8, name + "_scales")
+            nc.vector.quantize_mx(out=codes[:].bitcast(FP8X4), scales=scales[:], in_=woven[:])
+            return codes, scales
+
+        def cols(t):
+            return slice(t * P, (t + 1) * P)
+
+        w2_scale_raw = held([P, PASSES * H], U8, "w2_scale_raw")
+        nc.vector.memset(w2_scale_raw[:].bitcast(I32), 0)
+        tab_plane = held([P, T], U8, "tab_plane")
+        nc.gpsimd.memset(tab_plane[:].bitcast(I32), 0)
+        w4_scale_raw = held([P, H], U8, "w4_scale_raw")
+        nc.vector.memset(w4_scale_raw[:].bitcast(I32), 0)
+        v_plane1 = held([P, S], U8, "v_plane1")
+        nc.vector.memset(v_plane1[:].bitcast(I32), 0)
+
+        for q in range(QUADS):
+            nc.gpsimd.dma_start(
+                out=tab_plane[32 * q : 32 * q + 8, :].bitcast(I32),
+                in_=tab_scales[:, 4 * q : 4 * q + 4, :].bitcast(I32),
+            )
+
+        idx = keep.tile([P, S // 16], U16, name="idx")
+        nc.sync.dma_start(idx[:], offs)
+        tab = [held([P, T], U32, "tab%d" % a) for a in range(PASSES)]
+
+        def load_tab(a):
+            nc.sync.dma_start(
+                out=tab[a][:].bitcast(I32),
+                in_=tab_words[a].rearrange("p n i -> p (n i)").bitcast(I32),
+            )
+
+        w2_raw = held([P, PASSES * 2 * H], U8, "w2_raw")
+        nc.sync.dma_start(
+            out=w2_raw[:].bitcast(I32).rearrange("p (a c) -> p a c", a=PASSES),
+            in_=w2_words.rearrange("a p c -> p a c").bitcast(I32),
+        )
+        load_tab(0)
+        pos = keep.tile([P, M // 16], U16, name="pos")
+        nc.sync.dma_start(pos[:], pos1)
+        gain_t = held([P, PACK], F32, "gain_t")
+        nc.sync.dma_start(out=gain_t[:], in_=gain.rearrange("(p t) -> p t", t=PACK))
+        skip_t = held([P, PACK], F32, "skip_t")
+        nc.sync.dma_start(out=skip_t[:], in_=skip.rearrange("(p t) -> p t", t=PACK))
+        w4_raw = held([P, 2 * H], U8, "w4_raw")
+        nc.sync.dma_start(out=w4_raw[:].bitcast(I32), in_=w4_words[0].bitcast(I32))
+        for q in range(QUADS):
+            nc.scalar.dma_start(
+                out=w2_scale_raw[32 * q : 32 * q + 4, :].bitcast(I32).rearrange("r (a c) -> r a c", a=PASSES),
+                in_=w2_scales[:, 4 * q : 4 * q + 4, :].rearrange("a r c -> r a c").bitcast(I32),
+            )
+        w1_raw = [load_rows(w1[a * BANK : (a + 1) * BANK, :], "w1_raw%d" % a) for a in range(PASSES)]
+        load_tab(1)
+        w5_raw = [load_rows(w5[a * BANK : (a + 1) * BANK, :], "w5_raw%d" % a) for a in range(PASSES)]
+        tb = load_rows(timebase, "tb")
+        w3_raw = load_rows(w3, "w3_raw")
+        wg = held([P, PACK, M], F32, "wg")
+        for q in range(QUADS):
+            nc.sync.dma_start(
+                out=wg[32 * q : 32 * q + 32, :, :],
+                in_=wgo.rearrange("(p t) m -> p t m", t=PACK),
+            )
+
+        v_plane = held([P, S], U8, "v_plane")
+        nc.vector.tensor_copy(out=v_plane[:], in_=tab_plane[:].indirect(idx[:]))
+        for q in range(QUADS):
+            nc.gpsimd.dma_start(
+                out=v_plane1[32 * q : 32 * q + 4, :].bitcast(I32),
+                in_=v_plane[32 * q + 4 : 32 * q + 8, :].bitcast(I32),
+            )
+        for q in range(QUADS):
+            nc.gpsimd.dma_start(
+                out=w4_scale_raw[32 * q : 32 * q + 4, :].bitcast(I32),
+                in_=w4_scales[0, 4 * q : 4 * q + 4, :].bitcast(I32),
+            )
+
+        def deal_fp4(raw, scale_raw, passes, name):
+            codes = held([P, passes * 2 * H], U8, name + "_codes")
+            scales = held([P, passes * H], U8, name + "_scales")
+            nc.vector.tensor_copy(
+                out=codes[:].bitcast(U16).rearrange("p (a t m) -> p a m t", a=passes, t=PACK),
+                in_=raw[:].bitcast(U16).rearrange("p (a m t) -> p a m t", a=passes, t=PACK),
+            )
+            nc.vector.tensor_copy(
+                out=scales[:].rearrange("p (a t m) -> p a m t", a=passes, t=PACK),
+                in_=scale_raw[:].rearrange("p (a m t) -> p a m t", a=passes, t=PACK),
+            )
+            return codes, scales
+
+        def fp4_operand(weight, a, t):
+            c0 = a * H + t * P
+            return weight[0][:, 2 * c0 : 2 * (c0 + P)].bitcast(FP4X4), weight[1][:, c0 : c0 + P]
+
+        w2_q = deal_fp4(w2_raw, w2_scale_raw, PASSES, "w2")
+
+        v = [[held([P, BANK], U32, "v%d_%d" % (a, b)) for b in range(HALVES)] for a in range(PASSES)]
+
+        def gather_tab(a):
+            for b in range(HALVES):
+                piece = idx[:, b * BANK // 16 : (b + 1) * BANK // 16]
+                nc.vector.tensor_copy(out=v[a][b][:], in_=tab[a][:].indirect(piece))
+
+        gather_tab(0)
+        w1_q = [quantize(weave_weight(w1_raw[a]), "w1_%d" % a) for a in range(PASSES)]
+        w4_q = deal_fp4(w4_raw, w4_scale_raw, 1, "w4")
+        gather_tab(1)
+
+        def fp8_product(acc, weight, t, b):
+            for a in range(PASSES):
+                codes, scales = weight[a]
+                nc.tensor.matmul_mx(
+                    out=acc[:], lhsT=codes[:, cols(t)].bitcast(FP8X4), lhsT_scale=scales[:, cols(t)],
+                    rhs=v[a][b][:].bitcast(FP8X4), rhs_scale=v_plane[4 * a :, b * BANK : (b + 1) * BANK],
+                    start=(a == 0), stop=(a == PASSES - 1),
+                )
+
+        out_scale = held([P, PACK], F32, "out_scale")
+        nc.vector.tensor_tensor(out=out_scale[:], in0=gain_t[:], in1=skip_t[:], op=MULT)
+
+        u = [held([P, S], F32, "u%d" % t) for t in range(PACK)]
+        x_rows = held([P, PACK, M], BF16, "x_rows")
+        xt_rows = held([P, PACK, M], BF16, "xt_rows")
+
+        def stage1(t, b):
+            half = slice(b * BANK, (b + 1) * BANK)
+            bent_acc = psum.tile([P, BANK], F32, name="acc_a")
+            fp8_product(bent_acc, w1_q, t, b)
+            lin_acc = psum.tile([P, BANK], F32, name="acc_b")
+            for a in range(PASSES):
+                codes, scales = fp4_operand(w2_q, a, t)
+                nc.tensor.matmul_mx(
+                    out=lin_acc[:], lhsT=codes, lhsT_scale=scales,
+                    rhs=v[a][b][:].bitcast(FP8X4), rhs_scale=(v_plane, v_plane1)[a][:, half],
+                    start=(a == 0), stop=(a == PASSES - 1),
+                )
+            bent = ring.tile([P, BANK], F32, name="bent")
+            nc.scalar.activation(out=bent[:], in_=bent_acc[:], func=TANH)
+            nc.vector.tensor_tensor(out=u[t][:, half], in0=lin_acc[:], in1=bent[:], op=ADD)
+
+        def pick(t):
+            picked = keep.tile([P, M], F32, name="picked%d" % t)
+            nc.vector.tensor_copy(out=picked[:], in_=u[t][:].indirect(pos[:]))
+            nc.scalar.activation(out=x_rows[:, t, :], in_=picked[:], func=COPY, scale=gain_t[:, t : t + 1])
+            return picked
+
+        def times_timebase(t, picked):
+            nc.vector.scalar_tensor_tensor(
+                out=xt_rows[:, t, :], in0=picked[:], scalar=gain_t[:, t : t + 1], in1=tb[:, t, :],
+                op0=MULT, op1=MULT,
+            )
+
+        for t in (0, 2):
+            stage1(t, 0)
+            stage1(t + 1, 0)
+            stage1(t, 1)
+            stage1(t + 1, 1)
+            picks = [pick(t), pick(t + 1)]
+            times_timebase(t, picks[0])
+            times_timebase(t + 1, picks[1])
+
+        w3_q = quantize(weave_weight(w3_raw), "w3")
+
+        def weave_rows(rows, name):
+            woven = held([P, PACK * M], BF16, name)
+            nc.vector.tensor_copy(
+                out=woven[:].rearrange("p (c i t) -> p c t i", i=4, t=PACK),
+                in_=rows[:].rearrange("p t (c i) -> p c t i", i=4),
+            )
+            return woven
+
+        x_woven = weave_rows(x_rows, "x_woven")
+        xt_woven = weave_rows(xt_rows, "xt_woven")
+        x_q = quantize(x_woven, "x")
+        xt_q = quantize(xt_woven, "xt")
+        w5_q = [quantize(weave_weight(w5_raw[a]), "w5_%d" % a) for a in range(PASSES)]
+
+        out_rows = out.rearrange("(p t) j -> p t j", t=PACK)
+        for t in range(PACK):
+            d = held([P, S], F32, "d%d" % t)
+            for b in range(HALVES):
+                d_acc = psum.tile([P, BANK], F32, name="acc_b")
+                fp8_product(d_acc, w5_q, t, b)
+                nc.scalar.copy(out=d[:, b * BANK : (b + 1) * BANK], in_=d_acc[:])
+            page = held([P, S], F32, "page%d" % t)
+            nc.scalar.activation(out=page[:], in_=u[t][:], func=COPY, scale=out_scale[:, t : t + 1])
+            y_acc = psum.tile([P, M], F32, name="acc_a")
+            nc.tensor.matmul_mx(
+                out=y_acc[:], lhsT=w3_q[0][:, cols(t)].bitcast(FP8X4), lhsT_scale=w3_q[1][:, cols(t)],
+                rhs=x_q[0][:].bitcast(FP8X4), rhs_scale=x_q[1][:], start=True, stop=False,
+            )
+            codes, scales = fp4_operand(w4_q, 0, t)
+            nc.tensor.matmul_mx(
+                out=y_acc[:], lhsT=codes, lhsT_scale=scales,
+                rhs=xt_q[0][:].bitcast(FP8X4), rhs_scale=xt_q[1][:], start=False, stop=True,
+            )
+            y_bent = ring.tile([P, M], F32, name="y_bent")
+            nc.scalar.activation(out=y_bent[:], in_=y_acc[:], func=TANH)
+            y = ring.tile([P, M], F32, name="y")
+            nc.vector.tensor_tensor(out=y[:], in0=d[:].indirect(pos[:]), in1=y_bent[:], op=ADD)
+            nc.vector.tensor_tensor(out=page[:].indirect(pos[:]), in0=y[:], in1=wg[:, t, :], op=MULT)
+            nc.sync.dma_start(out=out_rows[:, t, :], in_=page[:])

@@ -44,12 +44,15 @@ def tile_list_chroma_line_restorer_kernel(
             nc.sync.dma_start(out=raw[:], in_=rows.rearrange("(p j) c -> p j c", j=PACK))
             return raw
 
-        def weave_weight(raw):
+        def pool_copy(out, in_):
+            nc.gpsimd.tensor_scalar(out=out, in0=in_, scalar1=1.0, scalar2=0.0, op0=MULT, op1=ADD)
+
+        def weave_weight(copy, raw):
             woven = ring.tile([P, PACK * H], BF16, name="weight_woven", align_bytes=64)
-            nc.scalar.copy(
-                out=woven[:].rearrange("p (t m j) -> p m j t", t=PACK, j=PACK),
-                in_=raw[:].rearrange("p j (m t) -> p m j t", t=PACK),
-            )
+            dst = woven[:].rearrange("p (t m j) -> p m j t", t=PACK, j=PACK)
+            src = raw[:].rearrange("p j (m t) -> p m j t", t=PACK)
+            for m0 in range(0, P, P // 2):
+                copy(out=dst[:, m0 : m0 + P // 2], in_=src[:, m0 : m0 + P // 2])
             return woven
 
         def quantize(woven, name):
@@ -61,20 +64,13 @@ def tile_list_chroma_line_restorer_kernel(
         def cols(t):
             return slice(t * P, (t + 1) * P)
 
+        tab_plane = held([P, PASSES * T], U8, "tab_plane")
+        nc.vector.memset(tab_plane[:, 0:T].bitcast(I32), 0)
+        nc.gpsimd.memset(tab_plane[:, T : 2 * T].bitcast(I32), 0)
         w2_scale_raw = held([P, PASSES * H], U8, "w2_scale_raw")
         nc.vector.memset(w2_scale_raw[:].bitcast(I32), 0)
-        tab_plane = held([P, T], U8, "tab_plane")
-        nc.gpsimd.memset(tab_plane[:].bitcast(I32), 0)
         w4_scale_raw = held([P, H], U8, "w4_scale_raw")
         nc.vector.memset(w4_scale_raw[:].bitcast(I32), 0)
-        v_plane1 = held([P, S], U8, "v_plane1")
-        nc.vector.memset(v_plane1[:].bitcast(I32), 0)
-
-        for q in range(QUADS):
-            nc.gpsimd.dma_start(
-                out=tab_plane[32 * q : 32 * q + 8, :].bitcast(I32),
-                in_=tab_scales[:, 4 * q : 4 * q + 4, :].bitcast(I32),
-            )
 
         idx = keep.tile([P, S // 16], U16, name="idx")
         nc.sync.dma_start(idx[:], offs)
@@ -86,28 +82,33 @@ def tile_list_chroma_line_restorer_kernel(
                 in_=tab_words[a].rearrange("p n i -> p (n i)").bitcast(I32),
             )
 
+        def load_scale_rows(plane, scales):
+            for q in range(QUADS):
+                nc.sync.dma_start(
+                    out=plane[32 * q : 32 * q + 4, :].bitcast(I32).rearrange("r (a c) -> r a c", a=scales.shape[0]),
+                    in_=scales[:, 4 * q : 4 * q + 4, :].rearrange("a r c -> r a c").bitcast(I32),
+                )
+
+        load_tab(0)
+        load_scale_rows(tab_plane, tab_scales)
         w2_raw = held([P, PASSES * 2 * H], U8, "w2_raw")
         nc.sync.dma_start(
             out=w2_raw[:].bitcast(I32).rearrange("p (a c) -> p a c", a=PASSES),
             in_=w2_words.rearrange("a p c -> p a c").bitcast(I32),
         )
-        load_tab(0)
+        w1_raw = [load_rows(w1[a * BANK : (a + 1) * BANK, :], "w1_raw%d" % a) for a in range(PASSES)]
+        load_scale_rows(w2_scale_raw, w2_scales)
+        w4_raw = held([P, 2 * H], U8, "w4_raw")
+        nc.sync.dma_start(out=w4_raw[:].bitcast(I32), in_=w4_words[0].bitcast(I32))
+        load_tab(1)
         pos = keep.tile([P, M // 16], U16, name="pos")
         nc.sync.dma_start(pos[:], pos1)
         gain_t = held([P, PACK], F32, "gain_t")
         nc.sync.dma_start(out=gain_t[:], in_=gain.rearrange("(p t) -> p t", t=PACK))
         skip_t = held([P, PACK], F32, "skip_t")
         nc.sync.dma_start(out=skip_t[:], in_=skip.rearrange("(p t) -> p t", t=PACK))
-        w4_raw = held([P, 2 * H], U8, "w4_raw")
-        nc.sync.dma_start(out=w4_raw[:].bitcast(I32), in_=w4_words[0].bitcast(I32))
-        for q in range(QUADS):
-            nc.scalar.dma_start(
-                out=w2_scale_raw[32 * q : 32 * q + 4, :].bitcast(I32).rearrange("r (a c) -> r a c", a=PASSES),
-                in_=w2_scales[:, 4 * q : 4 * q + 4, :].rearrange("a r c -> r a c").bitcast(I32),
-            )
-        w1_raw = [load_rows(w1[a * BANK : (a + 1) * BANK, :], "w1_raw%d" % a) for a in range(PASSES)]
-        load_tab(1)
         w5_raw = [load_rows(w5[a * BANK : (a + 1) * BANK, :], "w5_raw%d" % a) for a in range(PASSES)]
+        load_scale_rows(w4_scale_raw, w4_scales)
         tb = load_rows(timebase, "tb")
         w3_raw = load_rows(w3, "w3_raw")
         wg = held([P, PACK, M], F32, "wg")
@@ -117,18 +118,7 @@ def tile_list_chroma_line_restorer_kernel(
                 in_=wgo.rearrange("(p t) m -> p t m", t=PACK),
             )
 
-        v_plane = held([P, S], U8, "v_plane")
-        nc.vector.tensor_copy(out=v_plane[:], in_=tab_plane[:].indirect(idx[:]))
-        for q in range(QUADS):
-            nc.gpsimd.dma_start(
-                out=v_plane1[32 * q : 32 * q + 4, :].bitcast(I32),
-                in_=v_plane[32 * q + 4 : 32 * q + 8, :].bitcast(I32),
-            )
-        for q in range(QUADS):
-            nc.gpsimd.dma_start(
-                out=w4_scale_raw[32 * q : 32 * q + 4, :].bitcast(I32),
-                in_=w4_scales[0, 4 * q : 4 * q + 4, :].bitcast(I32),
-            )
+        v_plane = [held([P, S], U8, "v_plane%d" % a) for a in range(PASSES)]
 
         def deal_fp4(raw, scale_raw, passes, name):
             codes = held([P, passes * 2 * H], U8, name + "_codes")
@@ -147,7 +137,6 @@ def tile_list_chroma_line_restorer_kernel(
             c0 = a * H + t * P
             return weight[0][:, 2 * c0 : 2 * (c0 + P)].bitcast(FP4X4), weight[1][:, c0 : c0 + P]
 
-        w2_q = deal_fp4(w2_raw, w2_scale_raw, PASSES, "w2")
 
         v = [[held([P, BANK], U32, "v%d_%d" % (a, b)) for b in range(HALVES)] for a in range(PASSES)]
 
@@ -157,8 +146,10 @@ def tile_list_chroma_line_restorer_kernel(
                 nc.vector.tensor_copy(out=v[a][b][:], in_=tab[a][:].indirect(piece))
 
         gather_tab(0)
-        w1_q = [quantize(weave_weight(w1_raw[a]), "w1_%d" % a) for a in range(PASSES)]
-        w4_q = deal_fp4(w4_raw, w4_scale_raw, 1, "w4")
+        for a in range(PASSES):
+            nc.vector.tensor_copy(out=v_plane[a][:], in_=tab_plane[:, a * T : (a + 1) * T].indirect(idx[:]))
+        w2_q = deal_fp4(w2_raw, w2_scale_raw, PASSES, "w2")
+        w1_q = [quantize(weave_weight(nc.scalar.copy, w1_raw[a]), "w1_%d" % a) for a in range(PASSES)]
         gather_tab(1)
 
         def fp8_product(acc, weight, t, b):
@@ -166,7 +157,7 @@ def tile_list_chroma_line_restorer_kernel(
                 codes, scales = weight[a]
                 nc.tensor.matmul_mx(
                     out=acc[:], lhsT=codes[:, cols(t)].bitcast(FP8X4), lhsT_scale=scales[:, cols(t)],
-                    rhs=v[a][b][:].bitcast(FP8X4), rhs_scale=v_plane[4 * a :, b * BANK : (b + 1) * BANK],
+                    rhs=v[a][b][:].bitcast(FP8X4), rhs_scale=v_plane[a][:, b * BANK : (b + 1) * BANK],
                     start=(a == 0), stop=(a == PASSES - 1),
                 )
 
@@ -186,7 +177,7 @@ def tile_list_chroma_line_restorer_kernel(
                 codes, scales = fp4_operand(w2_q, a, t)
                 nc.tensor.matmul_mx(
                     out=lin_acc[:], lhsT=codes, lhsT_scale=scales,
-                    rhs=v[a][b][:].bitcast(FP8X4), rhs_scale=(v_plane, v_plane1)[a][:, half],
+                    rhs=v[a][b][:].bitcast(FP8X4), rhs_scale=v_plane[a][:, half],
                     start=(a == 0), stop=(a == PASSES - 1),
                 )
             bent = ring.tile([P, BANK], F32, name="bent")
@@ -194,7 +185,7 @@ def tile_list_chroma_line_restorer_kernel(
             nc.vector.tensor_tensor(out=u[t][:, half], in0=lin_acc[:], in1=bent[:], op=ADD)
 
         def pick(t):
-            picked = keep.tile([P, M], F32, name="picked%d" % t)
+            picked = held([P, M], F32, "picked%d" % t)
             nc.vector.tensor_copy(out=picked[:], in_=u[t][:].indirect(pos[:]))
             nc.scalar.activation(out=x_rows[:, t, :], in_=picked[:], func=COPY, scale=gain_t[:, t : t + 1])
             return picked
@@ -205,30 +196,32 @@ def tile_list_chroma_line_restorer_kernel(
                 op0=MULT, op1=MULT,
             )
 
+        picks = []
         for t in (0, 2):
             stage1(t, 0)
             stage1(t + 1, 0)
             stage1(t, 1)
             stage1(t + 1, 1)
-            picks = [pick(t), pick(t + 1)]
-            times_timebase(t, picks[0])
-            times_timebase(t + 1, picks[1])
+            picks.extend([pick(t), pick(t + 1)])
+        for t in range(PACK):
+            times_timebase(t, picks[t])
 
-        w3_q = quantize(weave_weight(w3_raw), "w3")
+        w5_q = [quantize(weave_weight(pool_copy, w5_raw[a]), "w5_%d" % a) for a in range(PASSES)]
+        w4_q = deal_fp4(w4_raw, w4_scale_raw, 1, "w4")
+        w3_q = quantize(weave_weight(nc.scalar.copy, w3_raw), "w3")
 
-        def weave_rows(rows, name):
+        def weave_rows(copy, rows, name):
             woven = held([P, PACK * M], BF16, name)
-            nc.vector.tensor_copy(
+            copy(
                 out=woven[:].rearrange("p (c i t) -> p c t i", i=4, t=PACK),
                 in_=rows[:].rearrange("p t (c i) -> p c t i", i=4),
             )
             return woven
 
-        x_woven = weave_rows(x_rows, "x_woven")
-        xt_woven = weave_rows(xt_rows, "xt_woven")
+        x_woven = weave_rows(nc.vector.tensor_copy, x_rows, "x_woven")
+        xt_woven = weave_rows(nc.scalar.copy, xt_rows, "xt_woven")
         x_q = quantize(x_woven, "x")
         xt_q = quantize(xt_woven, "xt")
-        w5_q = [quantize(weave_weight(w5_raw[a]), "w5_%d" % a) for a in range(PASSES)]
 
         out_rows = out.rearrange("(p t) j -> p t j", t=PACK)
         for t in range(PACK):
@@ -249,7 +242,7 @@ def tile_list_chroma_line_restorer_kernel(
                 out=y_acc[:], lhsT=codes, lhsT_scale=scales,
                 rhs=xt_q[0][:].bitcast(FP8X4), rhs_scale=xt_q[1][:], start=False, stop=True,
             )
-            y_bent = ring.tile([P, M], F32, name="y_bent")
+            y_bent = ring.tile([P, M], F32, name="bent")
             nc.scalar.activation(out=y_bent[:], in_=y_acc[:], func=TANH)
             y = ring.tile([P, M], F32, name="y")
             nc.vector.tensor_tensor(out=y[:], in0=d[:].indirect(pos[:]), in1=y_bent[:], op=ADD)

@@ -24,6 +24,7 @@ PASSES = K // (P * PACK)
 QUADS = 4
 BANK = 512
 HALVES = S // BANK
+XT_SPLIT = 64
 
 
 def tile_list_chroma_line_restorer_kernel(
@@ -44,15 +45,12 @@ def tile_list_chroma_line_restorer_kernel(
             nc.sync.dma_start(out=raw[:], in_=rows.rearrange("(p j) c -> p j c", j=PACK))
             return raw
 
-        def pool_copy(out, in_):
-            nc.gpsimd.tensor_scalar(out=out, in0=in_, scalar1=1.0, scalar2=0.0, op0=MULT, op1=ADD)
-
-        def weave_weight(copy, raw):
+        def weave_weight(raw):
             woven = ring.tile([P, PACK * H], BF16, name="weight_woven", align_bytes=64)
             dst = woven[:].rearrange("p (t m j) -> p m j t", t=PACK, j=PACK)
             src = raw[:].rearrange("p j (m t) -> p m j t", t=PACK)
             for m0 in range(0, P, P // 2):
-                copy(out=dst[:, m0 : m0 + P // 2], in_=src[:, m0 : m0 + P // 2])
+                nc.scalar.copy(out=dst[:, m0 : m0 + P // 2], in_=src[:, m0 : m0 + P // 2])
             return woven
 
         def quantize(woven, name):
@@ -83,23 +81,25 @@ def tile_list_chroma_line_restorer_kernel(
             )
 
         def load_scale_rows(plane, scales):
-            for q in range(QUADS):
+            for r in range(4):
                 nc.sync.dma_start(
-                    out=plane[32 * q : 32 * q + 4, :].bitcast(I32).rearrange("r (a c) -> r a c", a=scales.shape[0]),
-                    in_=scales[:, 4 * q : 4 * q + 4, :].rearrange("a r c -> r a c").bitcast(I32),
+                    out=plane[r:P:32, :].bitcast(I32).rearrange("q (a c) -> q a c", a=scales.shape[0]),
+                    in_=scales[:, r:16:4, :].rearrange("a q c -> q a c").bitcast(I32),
                 )
 
-        load_tab(0)
-        load_scale_rows(tab_plane, tab_scales)
         w2_raw = held([P, PASSES * 2 * H], U8, "w2_raw")
         nc.sync.dma_start(
             out=w2_raw[:].bitcast(I32).rearrange("p (a c) -> p a c", a=PASSES),
             in_=w2_words.rearrange("a p c -> p a c").bitcast(I32),
         )
-        w1_raw = [load_rows(w1[a * BANK : (a + 1) * BANK, :], "w1_raw%d" % a) for a in range(PASSES)]
-        load_scale_rows(w2_scale_raw, w2_scales)
         w4_raw = held([P, 2 * H], U8, "w4_raw")
         nc.sync.dma_start(out=w4_raw[:].bitcast(I32), in_=w4_words[0].bitcast(I32))
+        load_tab(0)
+        load_scale_rows(tab_plane, tab_scales)
+        w1_raw = [load_rows(w1[0:BANK, :], "w1_raw0")]
+        load_scale_rows(w2_scale_raw, w2_scales)
+        w1_raw.append(load_rows(w1[BANK : 2 * BANK, :], "w1_raw1"))
+        load_scale_rows(w4_scale_raw, w4_scales)
         load_tab(1)
         pos = keep.tile([P, M // 16], U16, name="pos")
         nc.sync.dma_start(pos[:], pos1)
@@ -108,7 +108,6 @@ def tile_list_chroma_line_restorer_kernel(
         skip_t = held([P, PACK], F32, "skip_t")
         nc.sync.dma_start(out=skip_t[:], in_=skip.rearrange("(p t) -> p t", t=PACK))
         w5_raw = [load_rows(w5[a * BANK : (a + 1) * BANK, :], "w5_raw%d" % a) for a in range(PASSES)]
-        load_scale_rows(w4_scale_raw, w4_scales)
         tb = load_rows(timebase, "tb")
         w3_raw = load_rows(w3, "w3_raw")
         wg = held([P, PACK, M], F32, "wg")
@@ -149,7 +148,8 @@ def tile_list_chroma_line_restorer_kernel(
         for a in range(PASSES):
             nc.vector.tensor_copy(out=v_plane[a][:], in_=tab_plane[:, a * T : (a + 1) * T].indirect(idx[:]))
         w2_q = deal_fp4(w2_raw, w2_scale_raw, PASSES, "w2")
-        w1_q = [quantize(weave_weight(nc.scalar.copy, w1_raw[a]), "w1_%d" % a) for a in range(PASSES)]
+        w1_q = [quantize(weave_weight(w1_raw[a]), "w1_%d" % a) for a in range(PASSES)]
+        w4_q = deal_fp4(w4_raw, w4_scale_raw, 1, "w4")
         gather_tab(1)
 
         def fp8_product(acc, weight, t, b):
@@ -165,8 +165,8 @@ def tile_list_chroma_line_restorer_kernel(
         nc.vector.tensor_tensor(out=out_scale[:], in0=gain_t[:], in1=skip_t[:], op=MULT)
 
         u = [held([P, S], F32, "u%d" % t) for t in range(PACK)]
-        x_rows = held([P, PACK, M], BF16, "x_rows")
-        xt_rows = held([P, PACK, M], BF16, "xt_rows")
+        x_rows = held([P, PACK * M], BF16, "d1")
+        xt_rows = held([P, PACK * M], BF16, "page1")
 
         def stage1(t, b):
             half = slice(b * BANK, (b + 1) * BANK)
@@ -187,12 +187,12 @@ def tile_list_chroma_line_restorer_kernel(
         def pick(t):
             picked = held([P, M], F32, "picked%d" % t)
             nc.vector.tensor_copy(out=picked[:], in_=u[t][:].indirect(pos[:]))
-            nc.scalar.activation(out=x_rows[:, t, :], in_=picked[:], func=COPY, scale=gain_t[:, t : t + 1])
+            nc.scalar.activation(out=x_rows[:, t * M : (t + 1) * M], in_=picked[:], func=COPY, scale=gain_t[:, t : t + 1])
             return picked
 
         def times_timebase(t, picked):
             nc.vector.scalar_tensor_tensor(
-                out=xt_rows[:, t, :], in0=picked[:], scalar=gain_t[:, t : t + 1], in1=tb[:, t, :],
+                out=xt_rows[:, t * M : (t + 1) * M], in0=picked[:], scalar=gain_t[:, t : t + 1], in1=tb[:, t, :],
                 op0=MULT, op1=MULT,
             )
 
@@ -206,31 +206,31 @@ def tile_list_chroma_line_restorer_kernel(
         for t in range(PACK):
             times_timebase(t, picks[t])
 
-        w5_q = [quantize(weave_weight(pool_copy, w5_raw[a]), "w5_%d" % a) for a in range(PASSES)]
-        w4_q = deal_fp4(w4_raw, w4_scale_raw, 1, "w4")
-        w3_q = quantize(weave_weight(nc.scalar.copy, w3_raw), "w3")
+        w5_q = [quantize(weave_weight(w5_raw[a]), "w5_%d" % a) for a in range(PASSES)]
+        w3_q = quantize(weave_weight(w3_raw), "w3")
 
-        def weave_rows(copy, rows, name):
-            woven = held([P, PACK * M], BF16, name)
+        def weave_rows(copy, woven, rows, c0, c1):
             copy(
-                out=woven[:].rearrange("p (c i t) -> p c t i", i=4, t=PACK),
-                in_=rows[:].rearrange("p t (c i) -> p c t i", i=4),
+                out=woven[:].rearrange("p (c i t) -> p c t i", i=4, t=PACK)[:, c0:c1],
+                in_=rows[:].rearrange("p (t c i) -> p c t i", i=4, t=PACK)[:, c0:c1],
             )
-            return woven
 
-        x_woven = weave_rows(nc.vector.tensor_copy, x_rows, "x_woven")
-        xt_woven = weave_rows(nc.scalar.copy, xt_rows, "xt_woven")
+        x_woven = held([P, PACK * M], BF16, "x_woven")
+        xt_woven = held([P, PACK * M], BF16, "xt_woven")
+        weave_rows(nc.vector.tensor_copy, x_woven, x_rows, 0, M // 4)
+        weave_rows(nc.vector.tensor_copy, xt_woven, xt_rows, 0, XT_SPLIT)
+        weave_rows(nc.scalar.copy, xt_woven, xt_rows, XT_SPLIT, M // 4)
         x_q = quantize(x_woven, "x")
         xt_q = quantize(xt_woven, "xt")
 
         out_rows = out.rearrange("(p t) j -> p t j", t=PACK)
         for t in range(PACK):
-            d = held([P, S], F32, "d%d" % t)
+            d = held([P, S], F32, "d%d" % (t % 2))
             for b in range(HALVES):
                 d_acc = psum.tile([P, BANK], F32, name="acc_b")
                 fp8_product(d_acc, w5_q, t, b)
                 nc.scalar.copy(out=d[:, b * BANK : (b + 1) * BANK], in_=d_acc[:])
-            page = held([P, S], F32, "page%d" % t)
+            page = held([P, S], F32, "page%d" % (t % 2))
             nc.scalar.activation(out=page[:], in_=u[t][:], func=COPY, scale=out_scale[:, t : t + 1])
             y_acc = psum.tile([P, M], F32, name="acc_a")
             nc.tensor.matmul_mx(

@@ -62,23 +62,32 @@ def tile_list_chroma_line_restorer_kernel(
         def cols(t):
             return slice(t * P, (t + 1) * P)
 
-        tab_plane = held([P, PASSES * T], U8, "tab_plane")
-        nc.vector.memset(tab_plane[:, 0:T].bitcast(I32), 0)
-        nc.gpsimd.memset(tab_plane[:, T : 2 * T].bitcast(I32), 0)
+        scale_rows = held([P, T], U8, "scale_rows")
+        nc.gpsimd.memset(scale_rows[32:64, :].bitcast(I32), 0)
+        nc.vector.memset(scale_rows[64:128, :].bitcast(I32), 0)
+        v_plane = [held([P, S], U8, "v_plane%d" % a) for a in range(PASSES)]
         w2_scale_raw = held([P, PASSES * H], U8, "w2_scale_raw")
         nc.vector.memset(w2_scale_raw[:].bitcast(I32), 0)
         w4_scale_raw = held([P, H], U8, "w4_scale_raw")
         nc.vector.memset(w4_scale_raw[:].bitcast(I32), 0)
 
+        for a in range(PASSES):
+            nc.vector.memset(v_plane[a][:].bitcast(I32), 0)
+
         idx = keep.tile([P, S // 16], U16, name="idx")
         nc.sync.dma_start(idx[:], offs)
-        tab = [held([P, T], U32, "tab%d" % a) for a in range(PASSES)]
+        nc.sync.dma_start(
+            out=scale_rows[0:32, :].bitcast(I32),
+            in_=tab_scales.rearrange("a q t -> (a q) t").bitcast(I32),
+        )
 
         def load_tab(a):
+            words = held([P, T], U32, "tab%d" % a)
             nc.sync.dma_start(
-                out=tab[a][:].bitcast(I32),
+                out=words[:].bitcast(I32),
                 in_=tab_words[a].rearrange("p n i -> p (n i)").bitcast(I32),
             )
+            return words
 
         def load_scale_rows(plane, scales):
             for r in range(4):
@@ -94,13 +103,11 @@ def tile_list_chroma_line_restorer_kernel(
         )
         w4_raw = held([P, 2 * H], U8, "w4_raw")
         nc.sync.dma_start(out=w4_raw[:].bitcast(I32), in_=w4_words[0].bitcast(I32))
-        load_tab(0)
-        load_scale_rows(tab_plane, tab_scales)
-        w1_raw = [load_rows(w1[0:BANK, :], "w1_raw0")]
+        tab0 = load_tab(0)
         load_scale_rows(w2_scale_raw, w2_scales)
-        w1_raw.append(load_rows(w1[BANK : 2 * BANK, :], "w1_raw1"))
+        w1_raw = [load_rows(w1[a * BANK : (a + 1) * BANK, :], "w1_raw%d" % a) for a in range(PASSES)]
         load_scale_rows(w4_scale_raw, w4_scales)
-        load_tab(1)
+        tab1 = load_tab(1)
         pos = keep.tile([P, M // 16], U16, name="pos")
         nc.sync.dma_start(pos[:], pos1)
         gain_t = held([P, PACK], F32, "gain_t")
@@ -117,20 +124,24 @@ def tile_list_chroma_line_restorer_kernel(
                 in_=wgo.rearrange("(p t) m -> p t m", t=PACK),
             )
 
-        v_plane = [held([P, S], U8, "v_plane%d" % a) for a in range(PASSES)]
+        v_rows = held([P, S], U8, "v_rows")
+        nc.vector.tensor_copy(out=v_rows[:], in_=scale_rows[:].indirect(idx[:]))
+        nc.vector.tensor_copy(out=v_plane[0][0:32, :].bitcast(I32), in_=v_rows[0:32, :].bitcast(I32))
 
-        def deal_fp4(raw, scale_raw, passes, name):
-            codes = held([P, passes * 2 * H], U8, name + "_codes")
-            scales = held([P, passes * H], U8, name + "_scales")
-            nc.vector.tensor_copy(
-                out=codes[:].bitcast(U16).rearrange("p (a t m) -> p a m t", a=passes, t=PACK),
-                in_=raw[:].bitcast(U16).rearrange("p (a m t) -> p a m t", a=passes, t=PACK),
+        for row in range(4, 32, 4):
+            a, q = divmod(row // 4, QUADS)
+            nc.gpsimd.dma_start(
+                out=v_plane[a][32 * q : 32 * q + 4, :].bitcast(I32),
+                in_=v_rows[row : row + 4, :].bitcast(I32),
             )
+
+        def deal(raw, dtype, name):
+            dealt = held(list(raw[:].shape), U8, name)
             nc.vector.tensor_copy(
-                out=scales[:].rearrange("p (a t m) -> p a m t", a=passes, t=PACK),
-                in_=scale_raw[:].rearrange("p (a m t) -> p a m t", a=passes, t=PACK),
+                out=dealt[:].bitcast(dtype).rearrange("p (a t m) -> p a m t", m=P, t=PACK),
+                in_=raw[:].bitcast(dtype).rearrange("p (a m t) -> p a m t", m=P, t=PACK),
             )
-            return codes, scales
+            return dealt
 
         def fp4_operand(weight, a, t):
             c0 = a * H + t * P
@@ -139,18 +150,16 @@ def tile_list_chroma_line_restorer_kernel(
 
         v = [[held([P, BANK], U32, "v%d_%d" % (a, b)) for b in range(HALVES)] for a in range(PASSES)]
 
-        def gather_tab(a):
+        def gather_tab(a, words):
             for b in range(HALVES):
                 piece = idx[:, b * BANK // 16 : (b + 1) * BANK // 16]
-                nc.vector.tensor_copy(out=v[a][b][:], in_=tab[a][:].indirect(piece))
+                nc.vector.tensor_copy(out=v[a][b][:], in_=words[:].indirect(piece))
 
-        gather_tab(0)
-        for a in range(PASSES):
-            nc.vector.tensor_copy(out=v_plane[a][:], in_=tab_plane[:, a * T : (a + 1) * T].indirect(idx[:]))
-        w2_q = deal_fp4(w2_raw, w2_scale_raw, PASSES, "w2")
+        w2_q = deal(w2_raw, U16, "w2_codes"), deal(w2_scale_raw, U8, "w2_scales")
+        gather_tab(0, tab0)
         w1_q = [quantize(weave_weight(w1_raw[a]), "w1_%d" % a) for a in range(PASSES)]
-        w4_q = deal_fp4(w4_raw, w4_scale_raw, 1, "w4")
-        gather_tab(1)
+        w4_q = deal(w4_raw, U16, "w4_codes"), deal(w4_scale_raw, U8, "w4_scales")
+        gather_tab(1, tab1)
 
         def fp8_product(acc, weight, t, b):
             for a in range(PASSES):

from contextlib import ExitStack

import concourse.mybir as mybir

K, H, T, S, M = 1024, 512, 4096, 1024, 512
FLOPS = 2 * (3 * K * H * S + 2 * H * H * M)

F32 = mybir.dt.float32
BF16 = mybir.dt.bfloat16
I32 = mybir.dt.int32
U32 = mybir.dt.uint32
U16 = mybir.dt.uint16
U8 = mybir.dt.uint8
FP8X4 = mybir.dt.float8_e4m3fn_x4
FP4X4 = mybir.dt.float4_e2m1fn_x4
ADD = mybir.AluOpType.add
MULT = mybir.AluOpType.mult
TANH = mybir.ActivationFunctionType.Tanh
COPY = mybir.ActivationFunctionType.Copy

P = 128
PACK = 4
PASSES = K // (P * PACK)
QUADS = 4
BANK = 512
HALVES = S // BANK
XT_SPLIT = 64


def tile_list_chroma_line_restorer_kernel(
    tc, tab_words, tab_scales, offs, pos1, w1, w2_words, w2_scales, gain, timebase,
    w3, w4_words, w4_scales, w5, skip, wgo, out,
):
    nc = tc.nc
    with ExitStack() as ctx:
        keep = ctx.enter_context(tc.tile_pool(name="keep", bufs=1))
        ring = ctx.enter_context(tc.tile_pool(name="ring", bufs=3))
        psum = ctx.enter_context(tc.psum_pool(name="psum", bufs=4))

        def held(shape, dtype, name):
            return keep.tile(shape, dtype, name=name, align_bytes=64)

        def load_rows(rows, name):
            raw = held([P, PACK, H], F32, name)
            nc.sync.dma_start(out=raw[:], in_=rows.rearrange("(p j) c -> p j c", j=PACK))
            return raw

        def weave_weight(raw):
            woven = ring.tile([P, PACK * H], BF16, name="weight_woven", align_bytes=64)
            dst = woven[:].rearrange("p (t m j) -> p m j t", t=PACK, j=PACK)
            src = raw[:].rearrange("p j (m t) -> p m j t", t=PACK)
            for m0 in range(0, P, P // 2):
                nc.scalar.copy(out=dst[:, m0 : m0 + P // 2], in_=src[:, m0 : m0 + P // 2])
            return woven

        def quantize(woven, name):
            codes = held([P, BANK], U32, name + "_codes")
            scales = held([P, BANK], U8, name + "_scales")
            nc.vector.quantize_mx(out=codes[:].bitcast(FP8X4), scales=scales[:], in_=woven[:])
            return codes, scales

        def cols(t):
            return slice(t * P, (t + 1) * P)

        scale_rows = held([P, T], U8, "scale_rows")
        nc.gpsimd.memset(scale_rows[32:64, :].bitcast(I32), 0)
        nc.vector.memset(scale_rows[64:128, :].bitcast(I32), 0)
        v_plane = [held([P, S], U8, "v_plane%d" % a) for a in range(PASSES)]
        w2_scale_raw = held([P, PASSES * H], U8, "w2_scale_raw")
        nc.vector.memset(w2_scale_raw[:].bitcast(I32), 0)
        w4_scale_raw = held([P, H], U8, "w4_scale_raw")
        nc.vector.memset(w4_scale_raw[:].bitcast(I32), 0)

        for a in range(PASSES):
            nc.vector.memset(v_plane[a][:].bitcast(I32), 0)

        idx = keep.tile([P, S // 16], U16, name="idx")
        nc.sync.dma_start(idx[:], offs)
        nc.sync.dma_start(
            out=scale_rows[0:32, :].bitcast(I32),
            in_=tab_scales.rearrange("a q t -> (a q) t").bitcast(I32),
        )

        def load_tab(a):
            words = held([P, T], U32, "tab%d" % a)
            nc.sync.dma_start(
                out=words[:].bitcast(I32),
                in_=tab_words[a].rearrange("p n i -> p (n i)").bitcast(I32),
            )
            return words

        def load_scale_rows(plane, scales):
            for r in range(4):
                nc.sync.dma_start(
                    out=plane[r:P:32, :].bitcast(I32).rearrange("q (a c) -> q a c", a=scales.shape[0]),
                    in_=scales[:, r:16:4, :].rearrange("a q c -> q a c").bitcast(I32),
                )

        w2_raw = held([P, PASSES * 2 * H], U8, "w2_raw")
        nc.sync.dma_start(
            out=w2_raw[:].bitcast(I32).rearrange("p (a c) -> p a c", a=PASSES),
            in_=w2_words.rearrange("a p c -> p a c").bitcast(I32),
        )
        w4_raw = held([P, 2 * H], U8, "w4_raw")
        nc.sync.dma_start(out=w4_raw[:].bitcast(I32), in_=w4_words[0].bitcast(I32))
        tab0 = load_tab(0)
        load_scale_rows(w2_scale_raw, w2_scales)
        w1_raw = [load_rows(w1[a * BANK : (a + 1) * BANK, :], "w1_raw%d" % a) for a in range(PASSES)]
        load_scale_rows(w4_scale_raw, w4_scales)
        tab1 = load_tab(1)
        pos = keep.tile([P, M // 16], U16, name="pos")
        nc.sync.dma_start(pos[:], pos1)
        gain_t = held([P, PACK], F32, "gain_t")
        nc.sync.dma_start(out=gain_t[:], in_=gain.rearrange("(p t) -> p t", t=PACK))
        skip_t = held([P, PACK], F32, "skip_t")
        nc.sync.dma_start(out=skip_t[:], in_=skip.rearrange("(p t) -> p t", t=PACK))
        w5_raw = [load_rows(w5[a * BANK : (a + 1) * BANK, :], "w5_raw%d" % a) for a in range(PASSES)]
        tb = load_rows(timebase, "tb")
        w3_raw = load_rows(w3, "w3_raw")
        wg = held([P, PACK, M], F32, "wg")
        for q in range(QUADS):
            nc.sync.dma_start(
                out=wg[32 * q : 32 * q + 32, :, :],
                in_=wgo.rearrange("(p t) m -> p t m", t=PACK),
            )

        v_rows = held([P, S], U8, "v_rows")
        nc.vector.tensor_copy(out=v_rows[:], in_=scale_rows[:].indirect(idx[:]))
        nc.vector.tensor_copy(out=v_plane[0][0:32, :].bitcast(I32), in_=v_rows[0:32, :].bitcast(I32))

        for row in range(4, 32, 4):
            a, q = divmod(row // 4, QUADS)
            nc.gpsimd.dma_start(
                out=v_plane[a][32 * q : 32 * q + 4, :].bitcast(I32),
                in_=v_rows[row : row + 4, :].bitcast(I32),
            )

        def deal(raw, dtype, name):
            dealt = held(list(raw[:].shape), U8, name)
            nc.vector.tensor_copy(
                out=dealt[:].bitcast(dtype).rearrange("p (a t m) -> p a m t", m=P, t=PACK),
                in_=raw[:].bitcast(dtype).rearrange("p (a m t) -> p a m t", m=P, t=PACK),
            )
            return dealt

        def fp4_operand(weight, a, t):
            c0 = a * H + t * P
            return weight[0][:, 2 * c0 : 2 * (c0 + P)].bitcast(FP4X4), weight[1][:, c0 : c0 + P]


        v = [[held([P, BANK], U32, "v%d_%d" % (a, b)) for b in range(HALVES)] for a in range(PASSES)]

        def gather_tab(a, words):
            for b in range(HALVES):
                piece = idx[:, b * BANK // 16 : (b + 1) * BANK // 16]
                nc.vector.tensor_copy(out=v[a][b][:], in_=words[:].indirect(piece))

        w2_q = deal(w2_raw, U16, "w2_codes"), deal(w2_scale_raw, U8, "w2_scales")
        gather_tab(0, tab0)
        w1_q = [quantize(weave_weight(w1_raw[a]), "w1_%d" % a) for a in range(PASSES)]
        w4_q = deal(w4_raw, U16, "w4_codes"), deal(w4_scale_raw, U8, "w4_scales")
        gather_tab(1, tab1)

        def fp8_product(acc, weight, t, b):
            for a in range(PASSES):
                codes, scales = weight[a]
                nc.tensor.matmul_mx(
                    out=acc[:], lhsT=codes[:, cols(t)].bitcast(FP8X4), lhsT_scale=scales[:, cols(t)],
                    rhs=v[a][b][:].bitcast(FP8X4), rhs_scale=v_plane[a][:, b * BANK : (b + 1) * BANK],
                    start=(a == 0), stop=(a == PASSES - 1),
                )

        out_scale = held([P, PACK], F32, "out_scale")
        nc.vector.tensor_tensor(out=out_scale[:], in0=gain_t[:], in1=skip_t[:], op=MULT)

        u = [held([P, S], F32, "u%d" % t) for t in range(PACK)]
        x_rows = held([P, PACK * M], BF16, "d1")
        xt_rows = held([P, PACK * M], BF16, "page1")

        def stage1(t, b):
            half = slice(b * BANK, (b + 1) * BANK)
            bent_acc = psum.tile([P, BANK], F32, name="acc_a")
            fp8_product(bent_acc, w1_q, t, b)
            lin_acc = psum.tile([P, BANK], F32, name="acc_b")
            for a in range(PASSES):
                codes, scales = fp4_operand(w2_q, a, t)
                nc.tensor.matmul_mx(
                    out=lin_acc[:], lhsT=codes, lhsT_scale=scales,
                    rhs=v[a][b][:].bitcast(FP8X4), rhs_scale=v_plane[a][:, half],
                    start=(a == 0), stop=(a == PASSES - 1),
                )
            bent = ring.tile([P, BANK], F32, name="bent")
            nc.scalar.activation(out=bent[:], in_=bent_acc[:], func=TANH)
            nc.vector.tensor_tensor(out=u[t][:, half], in0=lin_acc[:], in1=bent[:], op=ADD)

        def pick(t):
            picked = held([P, M], F32, "picked%d" % t)
            nc.vector.tensor_copy(out=picked[:], in_=u[t][:].indirect(pos[:]))
            nc.scalar.activation(out=x_rows[:, t * M : (t + 1) * M], in_=picked[:], func=COPY, scale=gain_t[:, t : t + 1])
            return picked

        def times_timebase(t, picked):
            nc.vector.scalar_tensor_tensor(
                out=xt_rows[:, t * M : (t + 1) * M], in0=picked[:], scalar=gain_t[:, t : t + 1], in1=tb[:, t, :],
                op0=MULT, op1=MULT,
            )

        picks = []
        for t in (0, 2):
            stage1(t, 0)
            stage1(t + 1, 0)
            stage1(t, 1)
            stage1(t + 1, 1)
            picks.extend([pick(t), pick(t + 1)])
        for t in range(PACK):
            times_timebase(t, picks[t])

        w5_q = [quantize(weave_weight(w5_raw[a]), "w5_%d" % a) for a in range(PASSES)]
        w3_q = quantize(weave_weight(w3_raw), "w3")

        def weave_rows(copy, woven, rows, c0, c1):
            copy(
                out=woven[:].rearrange("p (c i t) -> p c t i", i=4, t=PACK)[:, c0:c1],
                in_=rows[:].rearrange("p (t c i) -> p c t i", i=4, t=PACK)[:, c0:c1],
            )

        x_woven = held([P, PACK * M], BF16, "x_woven")
        xt_woven = held([P, PACK * M], BF16, "xt_woven")
        weave_rows(nc.vector.tensor_copy, x_woven, x_rows, 0, M // 4)
        weave_rows(nc.vector.tensor_copy, xt_woven, xt_rows, 0, XT_SPLIT)
        weave_rows(nc.scalar.copy, xt_woven, xt_rows, XT_SPLIT, M // 4)
        x_q = quantize(x_woven, "x")
        xt_q = quantize(xt_woven, "xt")

        out_rows = out.rearrange("(p t) j -> p t j", t=PACK)
        for t in range(PACK):
            d = held([P, S], F32, "d%d" % (t % 2))
            for b in range(HALVES):
                d_acc = psum.tile([P, BANK], F32, name="acc_b")
                fp8_product(d_acc, w5_q, t, b)
                nc.scalar.copy(out=d[:, b * BANK : (b + 1) * BANK], in_=d_acc[:])
            page = held([P, S], F32, "page%d" % (t % 2))
            nc.scalar.activation(out=page[:], in_=u[t][:], func=COPY, scale=out_scale[:, t : t + 1])
            y_acc = psum.tile([P, M], F32, name="acc_a")
            nc.tensor.matmul_mx(
                out=y_acc[:], lhsT=w3_q[0][:, cols(t)].bitcast(FP8X4), lhsT_scale=w3_q[1][:, cols(t)],
                rhs=x_q[0][:].bitcast(FP8X4), rhs_scale=x_q[1][:], start=True, stop=False,
            )
            codes, scales = fp4_operand(w4_q, 0, t)
            nc.tensor.matmul_mx(
                out=y_acc[:], lhsT=codes, lhsT_scale=scales,
                rhs=xt_q[0][:].bitcast(FP8X4), rhs_scale=xt_q[1][:], start=False, stop=True,
            )
            y_bent = ring.tile([P, M], F32, name="bent")
            nc.scalar.activation(out=y_bent[:], in_=y_acc[:], func=TANH)
            y = ring.tile([P, M], F32, name="y")
            nc.vector.tensor_tensor(out=y[:], in0=d[:].indirect(pos[:]), in1=y_bent[:], op=ADD)
            nc.vector.tensor_tensor(out=page[:].indirect(pos[:]), in0=y[:], in1=wg[:, t, :], op=MULT)
            nc.sync.dma_start(out=out_rows[:, t, :], in_=page[:])
